import numpy as np
import ml_dtypes


def mxq(x, axis, fmt="e4m3"):
    dtype, down = {"e4m3": (ml_dtypes.float8_e4m3fn, 7), "e5m2": (ml_dtypes.float8_e5m2, 14)}[fmt]
    v = np.moveaxis(np.asarray(x, np.float32).astype(ml_dtypes.bfloat16).astype(np.float64), axis, -1)
    blocks = v.reshape(v.shape[:-1] + (-1, 32))
    amax = np.abs(blocks).max(-1, keepdims=True)
    byte = np.maximum(np.where(amax > 0, np.frexp(amax)[1] - 1 + 127, 0) - down, 1)
    scale = np.exp2(byte - 127.0)
    codes = (blocks / scale).astype(np.float32).astype(dtype).astype(np.float64)
    return np.moveaxis((codes * scale).reshape(v.shape), -1, axis)


WIDE = False


def mx_kscale(k):
    if not WIDE:
        return np.ones(k)
    levels = np.array([10, -10, 5, -5, 0])
    if k % 512:
        return np.exp2(np.random.permutation(np.resize(levels, k // 32))).repeat(32)
    a = np.empty((k // 512, 16))
    for p in range(k // 512):
        a[p, :8] = np.random.permutation(np.resize(levels, 8))
        for g in range(8):
            far = levels[np.abs(levels - a[p, g]) >= 10]
            a[p, g + 8] = far[np.random.randint(len(far))]
    return np.exp2(a.ravel()).repeat(32)


def f64(x):
    return np.asarray(x).astype(np.float64)


def striped(idx):
    return np.tile(idx.reshape(-1, 16).T, (8, 1)).astype(np.uint16)


def unstriped(offs):
    return offs[:16].T.reshape(-1).astype(np.int64)


def silu(v):
    return v / (1.0 + np.exp(-np.maximum(v, -700.0)))


K, T, E, C, H, N = 512, 512, 4, 128, 1024, 512


def by_expert(wq, xq):
    return np.concatenate([wq[e].T @ xq[:, e * C:(e + 1) * C] for e in range(E)], axis=1)


def setup_inputs():
    n = np.random.standard_normal
    s = mx_kscale(K)[:, None]
    u = mx_kscale(H)
    return {
        "xT": (n((K, T)) * s).astype(np.float32),
        "w1": (n((E, K, H)) / np.sqrt(K) / s[None] * u[None, None, :]).astype(np.float32),
        "w2": (n((E, H, N)) / np.sqrt(H) / u[None, :, None]).astype(np.float32),
        "gate": np.tile(np.random.uniform(0.2, 1.0, E * C), (N, 1)).astype(np.float32),
        "offs": striped(np.random.permutation(T)[:E * C]),
    }


def reference(xT, w1, w2, gate, offs):
    idx = unstriped(offs)
    xq = mxq(f64(xT)[:, idx], 0, "e4m3")
    h = silu(by_expert(mxq(f64(w1), 1, "e4m3"), xq))
    y = by_expert(mxq(f64(w2), 1, "e4m3"), mxq(h, 0, "e4m3"))
    out = np.zeros((N, T))
    out[:, idx] = f64(gate) * y
    return out

@@ -1,0 +1,216 @@
+from contextlib import ExitStack
+
+import concourse.mybir as mybir
+
+K, T, E, C, H, N = 512, 512, 4, 128, 1024, 512
+FLOPS = 2 * E * C * (K * H + H * N)
+
+F32 = mybir.dt.float32
+BF16 = mybir.dt.bfloat16
+U32 = mybir.dt.uint32
+U16 = mybir.dt.uint16
+U8 = mybir.dt.uint8
+FP8X4 = mybir.dt.float8_e4m3fn_x4
+SILU = mybir.ActivationFunctionType.Silu
+MULT = mybir.AluOpType.mult
+ADD = mybir.AluOpType.add
+
+P = 128
+PACK = 4
+PASS = P * PACK
+HALVES = H // PASS
+NB = N // P
+GSLOTS = 256
+LINE = 4
+
+SHARES = (("v", 6), ("s", 10))
+SPLIT_W1 = (0, 3)
+LAST_PIECES = {0: 1, 1: 1, 2: 1, 3: 2}
+FORM = "d"
+GATE_AFTER = (1, 1)
+
+
+def tile_routed_moe_kernel(tc, xT, w1, w2, gate, offs, out):
+    nc = tc.nc
+    with ExitStack() as ctx:
+        held = ctx.enter_context(tc.tile_pool(name="held", bufs=1))
+        stage = ctx.enter_context(tc.tile_pool(name="stage", bufs=4))
+        small = ctx.enter_context(tc.tile_pool(name="small", bufs=2))
+        psum_a = ctx.enter_context(tc.psum_pool(name="psum_a", bufs=4))
+        psum_y = ctx.enter_context(tc.psum_pool(name="psum_y", bufs=3))
+
+        offsets = held.tile([P, T // 16], U16, name="offsets")
+        nc.sync.dma_start(offsets[:], offs)
+
+        x_rows = xT.rearrange("(p t) n -> p t n", t=PACK)
+        planes = []
+        for t in range(PACK):
+            plane = held.tile([P, T], F32, name="plane%d" % t)
+            nc.sync.dma_start(plane[:], x_rows[:, t, :])
+            planes.append(plane)
+
+        raw = {}
+        gate_sb = held.tile([P, NB, E * C], F32, name="gate_sb")
+        for e in range(E):
+            w1_rows = w1[e].rearrange("(p j) c -> p j c", j=PACK)
+            if e in SPLIT_W1:
+                for g in range(HALVES):
+                    r = held.tile([P, PACK, PASS], F32, name="raw1_%d_%d" % (e, g))
+                    nc.sync.dma_start(r[:], w1_rows[:, :, g * PASS:(g + 1) * PASS])
+                    raw[(e, 1, g)] = [r[:]]
+            else:
+                r = held.tile([P, PACK, H], F32, name="raw1_%d" % e)
+                nc.sync.dma_start(r[:], w1_rows)
+                for g in range(HALVES):
+                    raw[(e, 1, g)] = [r[:, :, g * PASS:(g + 1) * PASS]]
+            if GATE_AFTER == (1, e):
+                nc.sync.dma_start(gate_sb[:], gate.rearrange("(b p) j -> p b j", p=P))
+            for g in range(HALVES):
+                w2_rows = w2[e, g * PASS:(g + 1) * PASS, :].rearrange("(p j) n -> p j n", j=PACK)
+                pieces = LAST_PIECES[e] if g == HALVES - 1 else 1
+                width = N // pieces
+                raw[(e, 2, g)] = []
+                for i in range(pieces):
+                    r = held.tile([P, PACK, width], F32, name="raw2_%d_%d_%d" % (e, g, i))
+                    nc.sync.dma_start(r[:], w2_rows[:, :, i * width:(i + 1) * width])
+                    raw[(e, 2, g)].append(r[:])
+            if GATE_AFTER == (2, e):
+                nc.sync.dma_start(gate_sb[:], gate.rearrange("(b p) j -> p b j", p=P))
+
+        warm_in = held.tile([P, 1], F32, name="warm_in")
+        warm_out = held.tile([P, 1], F32, name="warm_out")
+        nc.vector.memset(warm_in[:], 0.0)
+        nc.scalar.activation(out=warm_out[:], in_=warm_in[:], func=SILU)
+
+        x_codes = []
+        x_scales = []
+        for hf in range(E * C // GSLOTS):
+            g4 = held.tile([P, PACK, GSLOTS], F32, name="g4_%d" % hf)
+            cols = slice(hf * GSLOTS // 16, (hf + 1) * GSLOTS // 16)
+            for t in range(PACK):
+                nc.vector.tensor_copy(g4[:, t, :], planes[t][:].indirect(offsets[:, cols]))
+            xg = held.tile([P, GSLOTS * PACK], BF16, name="xg_%d" % hf, align_bytes=64)
+            nc.vector.tensor_copy(
+                out=xg[:].rearrange("p (c i t) -> p c t i", i=LINE, t=PACK),
+                in_=g4[:].rearrange("p t (c i) -> p c t i", i=LINE),
+            )
+            xc = held.tile([P, GSLOTS], U32, name="xc_%d" % hf, align_bytes=64)
+            xs = held.tile([P, GSLOTS], U8, name="xs_%d" % hf, align_bytes=64)
+            nc.vector.quantize_mx(out=xc[:].bitcast(FP8X4), scales=xs[:], in_=xg[:])
+            x_codes.append(xc)
+            x_scales.append(xs)
+
+        def weights(e, layer, g, piece):
+            src = raw[(e, layer, g)][piece]
+            width = src.shape[2]
+            grouped = stage.tile([P, PACK * width], BF16, name="grouped", align_bytes=64)
+            if layer == 1:
+                dst_v = grouped[:].rearrange("p (t m j) -> p m j t", t=PACK, j=PACK)
+                src_v = src.rearrange("p j (m t) -> p m j t", t=PACK)
+                dst_g = grouped[:].rearrange("p (t m j) -> p m t j", t=PACK, j=PACK)
+                src_g = src.rearrange("p j (m t) -> p m t j", t=PACK)
+            else:
+                dst_v = grouped[:].rearrange("p (c i j) -> p c j i", i=LINE, j=PACK)
+                src_v = src.rearrange("p j (c i) -> p c j i", i=LINE)
+                dst_g = grouped[:].rearrange("p (c i j) -> p c i j", i=LINE, j=PACK)
+                src_g = src.rearrange("p j (c i) -> p c i j", i=LINE)
+            groups = width // LINE
+            lo = 0
+            for engine, share in SHARES:
+                hi = lo + groups * share // 16
+                if engine == "v":
+                    nc.vector.tensor_copy(out=dst_v[:, lo:hi], in_=src_v[:, lo:hi])
+                elif engine == "s":
+                    nc.scalar.copy(out=dst_v[:, lo:hi], in_=src_v[:, lo:hi])
+                else:
+                    nc.gpsimd.tensor_scalar(out=dst_g[:, lo:hi], in0=src_g[:, lo:hi], scalar1=1.0, scalar2=0.0, op0=MULT, op1=ADD)
+                lo = hi
+            codes = stage.tile([P, width], U32, name="codes", align_bytes=64)
+            scales = stage.tile([P, width], U8, name="scales", align_bytes=64)
+            nc.vector.quantize_mx(out=codes[:].bitcast(FP8X4), scales=scales[:], in_=grouped[:])
+            return codes, scales
+
+        windows = []
+        for b in range(NB):
+            win = held.tile([P, T], F32, name="win%d" % b)
+            windows.append(win)
+
+        hidden = {}
+        sums = {}
+
+        def layer_one(e):
+            xc = x_codes[e * C // GSLOTS]
+            xs = x_scales[e * C // GSLOTS]
+            sl = slice((e * C) % GSLOTS, (e * C) % GSLOTS + C)
+            hb = small.tile([P, HALVES, C, PACK], BF16, name="hb", align_bytes=64)
+            for g in range(HALVES):
+                wc, ws = weights(e, 1, g, 0)
+                a = psum_a.tile([P, PACK, C], F32, name="a")
+                for t in range(PACK):
+                    ms = slice(t * P, (t + 1) * P)
+                    nc.tensor.matmul_mx(
+                        out=a[:, t, :],
+                        lhsT=wc[:, ms].bitcast(FP8X4), lhsT_scale=ws[:, ms],
+                        rhs=xc[:, sl].bitcast(FP8X4), rhs_scale=xs[:, sl],
+                        start=True, stop=True,
+                    )
+                nc.scalar.activation(out=hb[:, g, :, :], in_=a[:].rearrange("p t n -> p n t"), func=SILU)
+            hc = small.tile([P, HALVES * C], U32, name="hc", align_bytes=64)
+            hs = small.tile([P, HALVES * C], U8, name="hs", align_bytes=64)
+            nc.vector.quantize_mx(out=hc[:].bitcast(FP8X4), scales=hs[:], in_=hb[:].rearrange("p g n t -> p (g n t)"))
+            hidden[e] = (hc, hs)
+
+        def way_back(e, i):
+            pieces = LAST_PIECES[e]
+            nb = NB // pieces
+            y = sums[(e, i)]
+            ocols = slice(e * C // 16, (e + 1) * C // 16)
+            ysb = small.tile([P, nb, C], F32, name="ysb")
+            if FORM == "d":
+                nc.scalar.copy(out=ysb[:], in_=y[:])
+            else:
+                nc.vector.tensor_tensor(out=ysb[:], in0=y[:], in1=gate_sb[:, i * nb:(i + 1) * nb, e * C:(e + 1) * C], op=MULT)
+            for k in range(nb):
+                b = i * nb + k
+                if FORM == "d":
+                    nc.vector.tensor_tensor(
+                        out=windows[b][:].indirect(offsets[:, ocols]),
+                        in0=ysb[:, k, :], in1=gate_sb[:, b, e * C:(e + 1) * C], op=MULT,
+                    )
+                else:
+                    nc.vector.tensor_copy(windows[b][:].indirect(offsets[:, ocols]), ysb[:, k, :])
+                if e == E - 1:
+                    nc.sync.dma_start(out[b * P:(b + 1) * P, :], windows[b][:])
+
+        def layer_two(e, finish):
+            hc, hs = hidden[e]
+            first_c, first_s = weights(e, 2, 0, 0)
+            pieces = LAST_PIECES[e]
+            nb = NB // pieces
+            for i in range(pieces):
+                last_c, last_s = weights(e, 2, 1, i)
+                y = psum_y.tile([P, nb, C], F32, name="y")
+                for k in range(nb):
+                    b = i * nb + k
+                    nc.tensor.matmul_mx(
+                        out=y[:, k, :],
+                        lhsT=first_c[:, b * P:(b + 1) * P].bitcast(FP8X4), lhsT_scale=first_s[:, b * P:(b + 1) * P],
+                        rhs=hc[:, 0:C].bitcast(FP8X4), rhs_scale=hs[:, 0:C],
+                        start=True, stop=False,
+                    )
+                    nc.tensor.matmul_mx(
+                        out=y[:, k, :],
+                        lhsT=last_c[:, k * P:(k + 1) * P].bitcast(FP8X4), lhsT_scale=last_s[:, k * P:(k + 1) * P],
+                        rhs=hc[:, C:2 * C].bitcast(FP8X4), rhs_scale=hs[:, C:2 * C],
+                        start=False, stop=True,
+                    )
+                sums[(e, i)] = y
+                if finish:
+                    way_back(e, i)
+
+        layer_one(0)
+        for e in range(E):
+            layer_two(e, e == E - 1)
+            if e + 1 < E:
+                layer_one(e + 1)
+                way_back(e, 0)

@@ -23,10 +23,10 @@ NB = N // P
 GSLOTS = 256
 LINE = 4
 
-SHARES = (("v", 6), ("s", 10))
+SHARES = {1: (("v", 6), ("s", 10)), 2: (("g", 4), ("g", 4), ("s", 8))}
 SPLIT_W1 = (0, 3)
 LAST_PIECES = {0: 1, 1: 1, 2: 1, 3: 2}
-FORM = "d"
+FORM = "e"
 GATE_AFTER = (1, 1)
 
 
@@ -116,7 +116,7 @@ def tile_routed_moe_kernel(tc, xT, w1, w2, gate, offs, out):
                 src_g = src.rearrange("p j (c i) -> p c i j", i=LINE)
             groups = width // LINE
             lo = 0
-            for engine, share in SHARES:
+            for engine, share in SHARES[layer]:
                 hi = lo + groups * share // 16
                 if engine == "v":
                     nc.vector.tensor_copy(out=dst_v[:, lo:hi], in_=src_v[:, lo:hi])

@@ -23,10 +23,11 @@ NB = N // P
 GSLOTS = 256
 LINE = 4
 
-SHARES = {1: (("v", 6), ("s", 10)), 2: (("g", 4), ("g", 4), ("s", 8))}
+VECTOR_CHUNKS = ((0, 2, 0), (1, 1, 0), (1, 2, 0), (2, 1, 0), (2, 2, 0), (3, 1, 0), (3, 2, 1))
+SPLIT_CHUNKS = ()
 SPLIT_W1 = (0, 3)
 LAST_PIECES = {0: 1, 1: 1, 2: 1, 3: 2}
-FORM = "e"
+FORM = "d"
 GATE_AFTER = (1, 1)
 
 
@@ -116,7 +117,7 @@ def tile_routed_moe_kernel(tc, xT, w1, w2, gate, offs, out):
                 src_g = src.rearrange("p j (c i) -> p c i j", i=LINE)
             groups = width // LINE
             lo = 0
-            for engine, share in SHARES[layer]:
+            for engine, share in ((("v", 6), ("s", 10)) if (e, layer, g) in SPLIT_CHUNKS else ((("v", 16),) if (e, layer, g) in VECTOR_CHUNKS else (("s", 16),))):
                 hi = lo + groups * share // 16
                 if engine == "v":
                     nc.vector.tensor_copy(out=dst_v[:, lo:hi], in_=src_v[:, lo:hi])

@@ -23,7 +23,7 @@ NB = N // P
 GSLOTS = 256
 LINE = 4
 
-VECTOR_CHUNKS = ((0, 2, 0), (1, 1, 0), (1, 2, 0), (2, 1, 0), (2, 2, 0), (3, 1, 0), (3, 2, 1))
+VECTOR_CHUNKS = ((1, 1, 0), (1, 2, 0), (2, 1, 0), (3, 1, 0), (3, 2, 1))
 SPLIT_CHUNKS = ()
 SPLIT_W1 = (0, 3)
 LAST_PIECES = {0: 1, 1: 1, 2: 1, 3: 2}

@@ -23,10 +23,10 @@ NB = N // P
 GSLOTS = 256
 LINE = 4
 
-VECTOR_CHUNKS = ((1, 1, 0), (1, 2, 0), (2, 1, 0), (3, 1, 0), (3, 2, 1))
+VECTOR_CHUNKS = ((0, 2, 0), (1, 1, 0), (1, 2, 0), (2, 1, 0), (2, 2, 0), (3, 1, 0), (3, 2, 1))
 SPLIT_CHUNKS = ()
-SPLIT_W1 = (0, 3)
-LAST_PIECES = {0: 1, 1: 1, 2: 1, 3: 2}
+SPLIT_W1 = (0, 1, 2, 3)
+LAST_PIECES = {0: 1, 1: 1, 2: 1, 3: 4}
 FORM = "d"
 GATE_AFTER = (1, 1)
 
@@ -37,8 +37,8 @@ def tile_routed_moe_kernel(tc, xT, w1, w2, gate, offs, out):
         held = ctx.enter_context(tc.tile_pool(name="held", bufs=1))
         stage = ctx.enter_context(tc.tile_pool(name="stage", bufs=4))
         small = ctx.enter_context(tc.tile_pool(name="small", bufs=2))
-        psum_a = ctx.enter_context(tc.psum_pool(name="psum_a", bufs=4))
-        psum_y = ctx.enter_context(tc.psum_pool(name="psum_y", bufs=3))
+        psum_a = ctx.enter_context(tc.psum_pool(name="psum_a", bufs=3))
+        psum_y = ctx.enter_context(tc.psum_pool(name="psum_y", bufs=4))
 
         offsets = held.tile([P, T // 16], U16, name="offsets")
         nc.sync.dma_start(offsets[:], offs)

@@ -23,7 +23,7 @@ NB = N // P
 GSLOTS = 256
 LINE = 4
 
-VECTOR_CHUNKS = ((0, 2, 0), (1, 1, 0), (1, 2, 0), (2, 1, 0), (2, 2, 0), (3, 1, 0), (3, 2, 1))
+VECTOR_CHUNKS = ((0, 2, 1), (1, 1, 1), (2, 1, 1), (3, 1, 1))
 SPLIT_CHUNKS = ()
 SPLIT_W1 = (0, 1, 2, 3)
 LAST_PIECES = {0: 1, 1: 1, 2: 1, 3: 4}

@@ -23,12 +23,12 @@ NB = N // P
 GSLOTS = 256
 LINE = 4
 
-VECTOR_CHUNKS = ((0, 2, 1), (1, 1, 1), (2, 1, 1), (3, 1, 1))
+VECTOR_CHUNKS = ((0, 2, 1), (1, 2, 1), (2, 2, 1), (3, 1, 1))
 SPLIT_CHUNKS = ()
 SPLIT_W1 = (0, 1, 2, 3)
 LAST_PIECES = {0: 1, 1: 1, 2: 1, 3: 4}
 FORM = "d"
-GATE_AFTER = (1, 1)
+GATE_BEFORE = {0: (0, 2, 1), 1: (1, 2, 1), 2: (2, 2, 1), 3: (3, 2, 1)}
 
 
 def tile_routed_moe_kernel(tc, xT, w1, w2, gate, offs, out):
@@ -51,11 +51,22 @@ def tile_routed_moe_kernel(tc, xT, w1, w2, gate, offs, out):
             planes.append(plane)
 
         raw = {}
-        gate_sb = held.tile([P, NB, E * C], F32, name="gate_sb")
+        gate_rows = gate.rearrange("(b p) j -> p b j", p=P)
+        gate_sb = []
+        for e in range(E):
+            gs = held.tile([P, NB, C], F32, name="gate_sb%d" % e)
+            gate_sb.append(gs)
+
+        def load_gate(chunk):
+            for e in range(E):
+                if GATE_BEFORE[e] == chunk:
+                    nc.sync.dma_start(gate_sb[e][:], gate_rows[:, :, e * C:(e + 1) * C])
+
         for e in range(E):
             w1_rows = w1[e].rearrange("(p j) c -> p j c", j=PACK)
             if e in SPLIT_W1:
                 for g in range(HALVES):
+                    load_gate((e, 1, g))
                     r = held.tile([P, PACK, PASS], F32, name="raw1_%d_%d" % (e, g))
                     nc.sync.dma_start(r[:], w1_rows[:, :, g * PASS:(g + 1) * PASS])
                     raw[(e, 1, g)] = [r[:]]
@@ -64,9 +75,8 @@ def tile_routed_moe_kernel(tc, xT, w1, w2, gate, offs, out):
                 nc.sync.dma_start(r[:], w1_rows)
                 for g in range(HALVES):
                     raw[(e, 1, g)] = [r[:, :, g * PASS:(g + 1) * PASS]]
-            if GATE_AFTER == (1, e):
-                nc.sync.dma_start(gate_sb[:], gate.rearrange("(b p) j -> p b j", p=P))
             for g in range(HALVES):
+                load_gate((e, 2, g))
                 w2_rows = w2[e, g * PASS:(g + 1) * PASS, :].rearrange("(p j) n -> p j n", j=PACK)
                 pieces = LAST_PIECES[e] if g == HALVES - 1 else 1
                 width = N // pieces
@@ -75,8 +85,8 @@ def tile_routed_moe_kernel(tc, xT, w1, w2, gate, offs, out):
                     r = held.tile([P, PACK, width], F32, name="raw2_%d_%d_%d" % (e, g, i))
                     nc.sync.dma_start(r[:], w2_rows[:, :, i * width:(i + 1) * width])
                     raw[(e, 2, g)].append(r[:])
-            if GATE_AFTER == (2, e):
-                nc.sync.dma_start(gate_sb[:], gate.rearrange("(b p) j -> p b j", p=P))
+
+        load_gate("end")
 
         warm_in = held.tile([P, 1], F32, name="warm_in")
         warm_out = held.tile([P, 1], F32, name="warm_out")
@@ -170,13 +180,13 @@ def tile_routed_moe_kernel(tc, xT, w1, w2, gate, offs, out):
             if FORM == "d":
                 nc.scalar.copy(out=ysb[:], in_=y[:])
             else:
-                nc.vector.tensor_tensor(out=ysb[:], in0=y[:], in1=gate_sb[:, i * nb:(i + 1) * nb, e * C:(e + 1) * C], op=MULT)
+                nc.vector.tensor_tensor(out=ysb[:], in0=y[:], in1=gate_sb[e][:, i * nb:(i + 1) * nb, :], op=MULT)
             for k in range(nb):
                 b = i * nb + k
                 if FORM == "d":
                     nc.vector.tensor_tensor(
                         out=windows[b][:].indirect(offsets[:, ocols]),
-                        in0=ysb[:, k, :], in1=gate_sb[:, b, e * C:(e + 1) * C], op=MULT,
+                        in0=ysb[:, k, :], in1=gate_sb[e][:, b, :], op=MULT,
                     )
                 else:
                     nc.vector.tensor_copy(windows[b][:].indirect(offsets[:, ocols]), ysb[:, k, :])

@@ -23,7 +23,7 @@ NB = N // P
 GSLOTS = 256
 LINE = 4
 
-VECTOR_CHUNKS = ((0, 2, 1), (1, 2, 1), (2, 2, 1), (3, 1, 1))
+VECTOR_CHUNKS = ((0, 2, 1), (1, 1, 1), (1, 2, 1), (2, 1, 1), (2, 2, 1), (3, 1, 1))
 SPLIT_CHUNKS = ()
 SPLIT_W1 = (0, 1, 2, 3)
 LAST_PIECES = {0: 1, 1: 1, 2: 1, 3: 4}

@@ -28,7 +28,7 @@ SPLIT_CHUNKS = ()
 SPLIT_W1 = (0, 1, 2, 3)
 LAST_PIECES = {0: 1, 1: 1, 2: 1, 3: 4}
 FORM = "d"
-GATE_BEFORE = {0: (0, 2, 1), 1: (1, 2, 1), 2: (2, 2, 1), 3: (3, 2, 1)}
+GATE_BEFORE = {0: (0, 2, 1), 1: (1, 2, 1), 2: (3, 2, 1), 3: (3, 2, 1)}
 
 
 def tile_routed_moe_kernel(tc, xT, w1, w2, gate, offs, out):

@@ -23,9 +23,9 @@ NB = N // P
 GSLOTS = 256
 LINE = 4
 
-VECTOR_CHUNKS = ((0, 2, 1), (1, 1, 1), (1, 2, 1), (2, 1, 1), (2, 2, 1), (3, 1, 1))
+VECTOR_CHUNKS = ((0, 1, 1), (0, 2, 1), (1, 1, 1), (1, 2, 1), (2, 1, 1), (2, 2, 1), (3, 1, 1))
 SPLIT_CHUNKS = ()
-SPLIT_W1 = (0, 1, 2, 3)
+SPLIT_W1 = (1, 2, 3)
 LAST_PIECES = {0: 1, 1: 1, 2: 1, 3: 4}
 FORM = "d"
 GATE_BEFORE = {0: (0, 2, 1), 1: (1, 2, 1), 2: (3, 2, 1), 3: (3, 2, 1)}

@@ -28,6 +28,7 @@ SPLIT_CHUNKS = ()
 SPLIT_W1 = (1, 2, 3)
 LAST_PIECES = {0: 1, 1: 1, 2: 1, 3: 4}
 FORM = "d"
+Y_SPLIT = (2,)
 GATE_BEFORE = {0: (0, 2, 1), 1: (1, 2, 1), 2: (3, 2, 1), 3: (3, 2, 1)}
 
 
@@ -172,7 +173,7 @@ def tile_routed_moe_kernel(tc, xT, w1, w2, gate, offs, out):
             hidden[e] = (hc, hs)
 
         def way_back(e, i):
-            pieces = LAST_PIECES[e]
+            pieces = NB if e in Y_SPLIT else LAST_PIECES[e]
             nb = NB // pieces
             y = sums[(e, i)]
             ocols = slice(e * C // 16, (e + 1) * C // 16)
@@ -196,6 +197,25 @@ def tile_routed_moe_kernel(tc, xT, w1, w2, gate, offs, out):
         def layer_two(e, finish):
             hc, hs = hidden[e]
             first_c, first_s = weights(e, 2, 0, 0)
+            if e in Y_SPLIT:
+                for b in range(NB):
+                    y = psum_y.tile([P, 1, C], F32, name="y")
+                    nc.tensor.matmul_mx(
+                        out=y[:, 0, :],
+                        lhsT=first_c[:, b * P:(b + 1) * P].bitcast(FP8X4), lhsT_scale=first_s[:, b * P:(b + 1) * P],
+                        rhs=hc[:, 0:C].bitcast(FP8X4), rhs_scale=hs[:, 0:C],
+                        start=True, stop=False,
+                    )
+                    sums[(e, b)] = y
+                last_c, last_s = weights(e, 2, 1, 0)
+                for b in range(NB):
+                    nc.tensor.matmul_mx(
+                        out=sums[(e, b)][:, 0, :],
+                        lhsT=last_c[:, b * P:(b + 1) * P].bitcast(FP8X4), lhsT_scale=last_s[:, b * P:(b + 1) * P],
+                        rhs=hc[:, C:2 * C].bitcast(FP8X4), rhs_scale=hs[:, C:2 * C],
+                        start=False, stop=True,
+                    )
+                return
             pieces = LAST_PIECES[e]
             nb = NB // pieces
             for i in range(pieces):
@@ -224,4 +244,5 @@ def tile_routed_moe_kernel(tc, xT, w1, w2, gate, offs, out):
             layer_two(e, e == E - 1)
             if e + 1 < E:
                 layer_one(e + 1)
-                way_back(e, 0)
+                for i in range(NB if e in Y_SPLIT else 1):
+                    way_back(e, i)

@@ -21,7 +21,7 @@ PASS = P * PACK
 HALVES = H // PASS
 NB = N // P
 GSLOTS = 256
-LINE = 4
+LINE = 8
 
 VECTOR_CHUNKS = ((0, 1, 1), (0, 2, 1), (1, 1, 1), (1, 2, 1), (2, 1, 1), (2, 2, 1), (3, 1, 1))
 SPLIT_CHUNKS = ()
@@ -126,7 +126,7 @@ def tile_routed_moe_kernel(tc, xT, w1, w2, gate, offs, out):
                 src_v = src.rearrange("p j (c i) -> p c j i", i=LINE)
                 dst_g = grouped[:].rearrange("p (c i j) -> p c i j", i=LINE, j=PACK)
                 src_g = src.rearrange("p j (c i) -> p c i j", i=LINE)
-            groups = width // LINE
+            groups = width // (PACK if layer == 1 else LINE)
             lo = 0
             for engine, share in ((("v", 6), ("s", 10)) if (e, layer, g) in SPLIT_CHUNKS else ((("v", 16),) if (e, layer, g) in VECTOR_CHUNKS else (("s", 16),))):
                 hi = lo + groups * share // 16

@@ -197,7 +197,7 @@ def tile_routed_moe_kernel(tc, xT, w1, w2, gate, offs, out):
         def layer_two(e, finish):
             hc, hs = hidden[e]
             first_c, first_s = weights(e, 2, 0, 0)
-            if e in Y_SPLIT:
+            if e in Y_SPLIT or e == E - 1:
                 for b in range(NB):
                     y = psum_y.tile([P, 1, C], F32, name="y")
                     nc.tensor.matmul_mx(
@@ -207,14 +207,20 @@ def tile_routed_moe_kernel(tc, xT, w1, w2, gate, offs, out):
                         start=True, stop=False,
                     )
                     sums[(e, b)] = y
-                last_c, last_s = weights(e, 2, 1, 0)
+                if e in Y_SPLIT:
+                    last_c, last_s = weights(e, 2, 1, 0)
                 for b in range(NB):
+                    if e not in Y_SPLIT:
+                        last_c, last_s = weights(e, 2, 1, b)
+                    k = b if e in Y_SPLIT else 0
                     nc.tensor.matmul_mx(
                         out=sums[(e, b)][:, 0, :],
-                        lhsT=last_c[:, b * P:(b + 1) * P].bitcast(FP8X4), lhsT_scale=last_s[:, b * P:(b + 1) * P],
+                        lhsT=last_c[:, k * P:(k + 1) * P].bitcast(FP8X4), lhsT_scale=last_s[:, k * P:(k + 1) * P],
                         rhs=hc[:, C:2 * C].bitcast(FP8X4), rhs_scale=hs[:, C:2 * C],
                         start=False, stop=True,
                     )
+                    if finish:
+                        way_back(e, b)
                 return
             pieces = LAST_PIECES[e]
             nb = NB // pieces

from contextlib import ExitStack

import concourse.mybir as mybir

K, T, E, C, H, N = 512, 512, 4, 128, 1024, 512
FLOPS = 2 * E * C * (K * H + H * N)

F32 = mybir.dt.float32
BF16 = mybir.dt.bfloat16
U32 = mybir.dt.uint32
U16 = mybir.dt.uint16
U8 = mybir.dt.uint8
FP8X4 = mybir.dt.float8_e4m3fn_x4
SILU = mybir.ActivationFunctionType.Silu
MULT = mybir.AluOpType.mult
ADD = mybir.AluOpType.add

P = 128
PACK = 4
PASS = P * PACK
HALVES = H // PASS
NB = N // P
GSLOTS = 256
LINE = 8

VECTOR_CHUNKS = ((0, 1, 1), (0, 2, 1), (1, 1, 1), (1, 2, 1), (2, 1, 1), (2, 2, 1), (3, 1, 1))
SPLIT_CHUNKS = ()
SPLIT_W1 = (1, 2, 3)
LAST_PIECES = {0: 1, 1: 1, 2: 1, 3: 4}
FORM = "d"
Y_SPLIT = (2,)
GATE_BEFORE = {0: (0, 2, 1), 1: (1, 2, 1), 2: (3, 2, 1), 3: (3, 2, 1)}


def tile_routed_moe_kernel(tc, xT, w1, w2, gate, offs, out):
    nc = tc.nc
    with ExitStack() as ctx:
        held = ctx.enter_context(tc.tile_pool(name="held", bufs=1))
        stage = ctx.enter_context(tc.tile_pool(name="stage", bufs=4))
        small = ctx.enter_context(tc.tile_pool(name="small", bufs=2))
        psum_a = ctx.enter_context(tc.psum_pool(name="psum_a", bufs=3))
        psum_y = ctx.enter_context(tc.psum_pool(name="psum_y", bufs=4))

        offsets = held.tile([P, T // 16], U16, name="offsets")
        nc.sync.dma_start(offsets[:], offs)

        x_rows = xT.rearrange("(p t) n -> p t n", t=PACK)
        planes = []
        for t in range(PACK):
            plane = held.tile([P, T], F32, name="plane%d" % t)
            nc.sync.dma_start(plane[:], x_rows[:, t, :])
            planes.append(plane)

        raw = {}
        gate_rows = gate.rearrange("(b p) j -> p b j", p=P)
        gate_sb = []
        for e in range(E):
            gs = held.tile([P, NB, C], F32, name="gate_sb%d" % e)
            gate_sb.append(gs)

        def load_gate(chunk):
            for e in range(E):
                if GATE_BEFORE[e] == chunk:
                    nc.sync.dma_start(gate_sb[e][:], gate_rows[:, :, e * C:(e + 1) * C])

        for e in range(E):
            w1_rows = w1[e].rearrange("(p j) c -> p j c", j=PACK)
            if e in SPLIT_W1:
                for g in range(HALVES):
                    load_gate((e, 1, g))
                    r = held.tile([P, PACK, PASS], F32, name="raw1_%d_%d" % (e, g))
                    nc.sync.dma_start(r[:], w1_rows[:, :, g * PASS:(g + 1) * PASS])
                    raw[(e, 1, g)] = [r[:]]
            else:
                r = held.tile([P, PACK, H], F32, name="raw1_%d" % e)
                nc.sync.dma_start(r[:], w1_rows)
                for g in range(HALVES):
                    raw[(e, 1, g)] = [r[:, :, g * PASS:(g + 1) * PASS]]
            for g in range(HALVES):
                load_gate((e, 2, g))
                w2_rows = w2[e, g * PASS:(g + 1) * PASS, :].rearrange("(p j) n -> p j n", j=PACK)
                pieces = LAST_PIECES[e] if g == HALVES - 1 else 1
                width = N // pieces
                raw[(e, 2, g)] = []
                for i in range(pieces):
                    r = held.tile([P, PACK, width], F32, name="raw2_%d_%d_%d" % (e, g, i))
                    nc.sync.dma_start(r[:], w2_rows[:, :, i * width:(i + 1) * width])
                    raw[(e, 2, g)].append(r[:])

        load_gate("end")

        warm_in = held.tile([P, 1], F32, name="warm_in")
        warm_out = held.tile([P, 1], F32, name="warm_out")
        nc.vector.memset(warm_in[:], 0.0)
        nc.scalar.activation(out=warm_out[:], in_=warm_in[:], func=SILU)

        x_codes = []
        x_scales = []
        for hf in range(E * C // GSLOTS):
            g4 = held.tile([P, PACK, GSLOTS], F32, name="g4_%d" % hf)
            cols = slice(hf * GSLOTS // 16, (hf + 1) * GSLOTS // 16)
            for t in range(PACK):
                nc.vector.tensor_copy(g4[:, t, :], planes[t][:].indirect(offsets[:, cols]))
            xg = held.tile([P, GSLOTS * PACK], BF16, name="xg_%d" % hf, align_bytes=64)
            nc.vector.tensor_copy(
                out=xg[:].rearrange("p (c i t) -> p c t i", i=LINE, t=PACK),
                in_=g4[:].rearrange("p t (c i) -> p c t i", i=LINE),
            )
            xc = held.tile([P, GSLOTS], U32, name="xc_%d" % hf, align_bytes=64)
            xs = held.tile([P, GSLOTS], U8, name="xs_%d" % hf, align_bytes=64)
            nc.vector.quantize_mx(out=xc[:].bitcast(FP8X4), scales=xs[:], in_=xg[:])
            x_codes.append(xc)
            x_scales.append(xs)

        def weights(e, layer, g, piece):
            src = raw[(e, layer, g)][piece]
            width = src.shape[2]
            grouped = stage.tile([P, PACK * width], BF16, name="grouped", align_bytes=64)
            if layer == 1:
                dst_v = grouped[:].rearrange("p (t m j) -> p m j t", t=PACK, j=PACK)
                src_v = src.rearrange("p j (m t) -> p m j t", t=PACK)
                dst_g = grouped[:].rearrange("p (t m j) -> p m t j", t=PACK, j=PACK)
                src_g = src.rearrange("p j (m t) -> p m t j", t=PACK)
            else:
                dst_v = grouped[:].rearrange("p (c i j) -> p c j i", i=LINE, j=PACK)
                src_v = src.rearrange("p j (c i) -> p c j i", i=LINE)
                dst_g = grouped[:].rearrange("p (c i j) -> p c i j", i=LINE, j=PACK)
                src_g = src.rearrange("p j (c i) -> p c i j", i=LINE)
            groups = width // (PACK if layer == 1 else LINE)
            lo = 0
            for engine, share in ((("v", 6), ("s", 10)) if (e, layer, g) in SPLIT_CHUNKS else ((("v", 16),) if (e, layer, g) in VECTOR_CHUNKS else (("s", 16),))):
                hi = lo + groups * share // 16
                if engine == "v":
                    nc.vector.tensor_copy(out=dst_v[:, lo:hi], in_=src_v[:, lo:hi])
                elif engine == "s":
                    nc.scalar.copy(out=dst_v[:, lo:hi], in_=src_v[:, lo:hi])
                else:
                    nc.gpsimd.tensor_scalar(out=dst_g[:, lo:hi], in0=src_g[:, lo:hi], scalar1=1.0, scalar2=0.0, op0=MULT, op1=ADD)
                lo = hi
            codes = stage.tile([P, width], U32, name="codes", align_bytes=64)
            scales = stage.tile([P, width], U8, name="scales", align_bytes=64)
            nc.vector.quantize_mx(out=codes[:].bitcast(FP8X4), scales=scales[:], in_=grouped[:])
            return codes, scales

        windows = []
        for b in range(NB):
            win = held.tile([P, T], F32, name="win%d" % b)
            windows.append(win)

        hidden = {}
        sums = {}

        def layer_one(e):
            xc = x_codes[e * C // GSLOTS]
            xs = x_scales[e * C // GSLOTS]
            sl = slice((e * C) % GSLOTS, (e * C) % GSLOTS + C)
            hb = small.tile([P, HALVES, C, PACK], BF16, name="hb", align_bytes=64)
            for g in range(HALVES):
                wc, ws = weights(e, 1, g, 0)
                a = psum_a.tile([P, PACK, C], F32, name="a")
                for t in range(PACK):
                    ms = slice(t * P, (t + 1) * P)
                    nc.tensor.matmul_mx(
                        out=a[:, t, :],
                        lhsT=wc[:, ms].bitcast(FP8X4), lhsT_scale=ws[:, ms],
                        rhs=xc[:, sl].bitcast(FP8X4), rhs_scale=xs[:, sl],
                        start=True, stop=True,
                    )
                nc.scalar.activation(out=hb[:, g, :, :], in_=a[:].rearrange("p t n -> p n t"), func=SILU)
            hc = small.tile([P, HALVES * C], U32, name="hc", align_bytes=64)
            hs = small.tile([P, HALVES * C], U8, name="hs", align_bytes=64)
            nc.vector.quantize_mx(out=hc[:].bitcast(FP8X4), scales=hs[:], in_=hb[:].rearrange("p g n t -> p (g n t)"))
            hidden[e] = (hc, hs)

        def way_back(e, i):
            pieces = NB if e in Y_SPLIT else LAST_PIECES[e]
            nb = NB // pieces
            y = sums[(e, i)]
            ocols = slice(e * C // 16, (e + 1) * C // 16)
            ysb = small.tile([P, nb, C], F32, name="ysb")
            if FORM == "d":
                nc.scalar.copy(out=ysb[:], in_=y[:])
            else:
                nc.vector.tensor_tensor(out=ysb[:], in0=y[:], in1=gate_sb[e][:, i * nb:(i + 1) * nb, :], op=MULT)
            for k in range(nb):
                b = i * nb + k
                if FORM == "d":
                    nc.vector.tensor_tensor(
                        out=windows[b][:].indirect(offsets[:, ocols]),
                        in0=ysb[:, k, :], in1=gate_sb[e][:, b, :], op=MULT,
                    )
                else:
                    nc.vector.tensor_copy(windows[b][:].indirect(offsets[:, ocols]), ysb[:, k, :])
                if e == E - 1:
                    nc.sync.dma_start(out[b * P:(b + 1) * P, :], windows[b][:])

        def layer_two(e, finish):
            hc, hs = hidden[e]
            first_c, first_s = weights(e, 2, 0, 0)
            if e in Y_SPLIT or e == E - 1:
                for b in range(NB):
                    y = psum_y.tile([P, 1, C], F32, name="y")
                    nc.tensor.matmul_mx(
                        out=y[:, 0, :],
                        lhsT=first_c[:, b * P:(b + 1) * P].bitcast(FP8X4), lhsT_scale=first_s[:, b * P:(b + 1) * P],
                        rhs=hc[:, 0:C].bitcast(FP8X4), rhs_scale=hs[:, 0:C],
                        start=True, stop=False,
                    )
                    sums[(e, b)] = y
                if e in Y_SPLIT:
                    last_c, last_s = weights(e, 2, 1, 0)
                for b in range(NB):
                    if e not in Y_SPLIT:
                        last_c, last_s = weights(e, 2, 1, b)
                    k = b if e in Y_SPLIT else 0
                    nc.tensor.matmul_mx(
                        out=sums[(e, b)][:, 0, :],
                        lhsT=last_c[:, k * P:(k + 1) * P].bitcast(FP8X4), lhsT_scale=last_s[:, k * P:(k + 1) * P],
                        rhs=hc[:, C:2 * C].bitcast(FP8X4), rhs_scale=hs[:, C:2 * C],
                        start=False, stop=True,
                    )
                    if finish:
                        way_back(e, b)
                return
            pieces = LAST_PIECES[e]
            nb = NB // pieces
            for i in range(pieces):
                last_c, last_s = weights(e, 2, 1, i)
                y = psum_y.tile([P, nb, C], F32, name="y")
                for k in range(nb):
                    b = i * nb + k
                    nc.tensor.matmul_mx(
                        out=y[:, k, :],
                        lhsT=first_c[:, b * P:(b + 1) * P].bitcast(FP8X4), lhsT_scale=first_s[:, b * P:(b + 1) * P],
                        rhs=hc[:, 0:C].bitcast(FP8X4), rhs_scale=hs[:, 0:C],
                        start=True, stop=False,
                    )
                    nc.tensor.matmul_mx(
                        out=y[:, k, :],
                        lhsT=last_c[:, k * P:(k + 1) * P].bitcast(FP8X4), lhsT_scale=last_s[:, k * P:(k + 1) * P],
                        rhs=hc[:, C:2 * C].bitcast(FP8X4), rhs_scale=hs[:, C:2 * C],
                        start=False, stop=True,
                    )
                sums[(e, i)] = y
                if finish:
                    way_back(e, i)

        layer_one(0)
        for e in range(E):
            layer_two(e, e == E - 1)
            if e + 1 < E:
                layer_one(e + 1)
                for i in range(NB if e in Y_SPLIT else 1):
                    way_back(e, i)
